import numpy as np
import ml_dtypes


def mxq(x, axis, fmt="e4m3"):
    dtype, down = {"e4m3": (ml_dtypes.float8_e4m3fn, 7), "e5m2": (ml_dtypes.float8_e5m2, 14)}[fmt]
    v = np.moveaxis(np.asarray(x, np.float32).astype(ml_dtypes.bfloat16).astype(np.float64), axis, -1)
    blocks = v.reshape(v.shape[:-1] + (-1, 32))
    amax = np.abs(blocks).max(-1, keepdims=True)
    byte = np.maximum(np.where(amax > 0, np.frexp(amax)[1] - 1 + 127, 0) - down, 1)
    scale = np.exp2(byte - 127.0)
    codes = (blocks / scale).astype(np.float32).astype(dtype).astype(np.float64)
    return np.moveaxis((codes * scale).reshape(v.shape), -1, axis)


WIDE = False


def mx_kscale(k):
    if not WIDE:
        return np.ones(k)
    levels = np.array([10, -10, 5, -5, 0])
    if k % 512:
        return np.exp2(np.random.permutation(np.resize(levels, k // 32))).repeat(32)
    a = np.empty((k // 512, 16))
    for p in range(k // 512):
        a[p, :8] = np.random.permutation(np.resize(levels, 8))
        for g in range(8):
            far = levels[np.abs(levels - a[p, g]) >= 10]
            a[p, g + 8] = far[np.random.randint(len(far))]
    return np.exp2(a.ravel()).repeat(32)


def f64(x):
    return np.asarray(x).astype(np.float64)


def striped(idx):
    return np.tile(np.asarray(idx).reshape(-1, 16).T, (8, 1)).astype(np.uint16)


def unstriped(offs):
    return offs[:16].T.reshape(-1).astype(np.int64)


G, K, T, D, M = 64, 16, 2048, 512, 256


def setup_inputs():
    n = np.random.standard_normal
    s = mx_kscale(D)[:, None]
    x = n((D, T)) * s
    idx = np.stack([np.random.permutation(T)[:K] for g in range(G)])
    return {
        "xT": x.astype(np.float32),
        "w": (n((D, M)) / np.sqrt(D) / s).astype(np.float32),
        "offs": striped(idx.reshape(-1)),
    }


def reference(xT, w, offs):
    x = f64(xT)[:, unstriped(offs)]
    y = (mxq(f64(w), 0, "e4m3").T @ mxq(x, 0, "e4m3")).reshape(M, G, K).max(-1)
    return y

@@ -1,0 +1,115 @@
+from contextlib import ExitStack
+
+import concourse.mybir as mybir
+
+D, T, M = 512, 2048, 256
+G, NB = 64, 16
+E = G * NB
+P = 128
+FLOPS = 2 * D * M * E
+
+F32 = mybir.dt.float32
+BF16 = mybir.dt.bfloat16
+U32 = mybir.dt.uint32
+U16 = mybir.dt.uint16
+U8 = mybir.dt.uint8
+FP8X4 = mybir.dt.float8_e4m3fn_x4
+COPY = mybir.ActivationFunctionType.Copy
+MAX = mybir.AluOpType.max
+AXIS_X = mybir.AxisListType.X
+
+HALVES = 2
+EH = E // HALVES
+GH = G // HALVES
+
+
+def tile_attend_edge_kernel(tc, xT, w, offs, out):
+    nc = tc.nc
+    x_rows = xT.rearrange("(p j) t -> p j t", j=4)
+    w_rows = w.rearrange("(p j) m -> p j m", j=4)
+    out_rows = out.rearrange("(a p) g -> p a g", p=P)
+
+    chunks = [
+        (0, 0, 1024, 640),
+        (0, 1024, 1024, 640),
+        (1, 0, 1024, 640),
+        (1, 1024, 512, 320),
+        (1, 1536, 512, 320),
+    ]
+
+    with ExitStack() as ctx:
+        keep = ctx.enter_context(tc.tile_pool(name="keep", bufs=1))
+        psum = ctx.enter_context(tc.psum_pool(name="psum", bufs=1))
+
+        lists = keep.tile([P, E // 16], U16, name="lists")
+        w_raw = keep.tile([P, 4, M], F32, name="w_raw")
+        raw = []
+        for i, (u, c0, n, nv) in enumerate(chunks):
+            r = keep.tile([P, 2, n], F32, name=f"raw{i}")
+            raw.append(r)
+            nc.sync.dma_start(r[:], x_rows[:, 2 * u : 2 * u + 2, c0 : c0 + n])
+            if i == 0:
+                nc.sync.dma_start(lists[:], offs)
+            if i == 1:
+                nc.sync.dma_start(w_raw[:], w_rows)
+
+        pairs = [keep.tile([P, T, 2], BF16, name=f"pairs{u}") for u in range(2)]
+        words = [t[:].rearrange("p t e -> p (t e)").bitcast(U32) for t in pairs]
+
+        def cast(i):
+            u, c0, n, nv = chunks[i]
+            nc.vector.tensor_copy(
+                pairs[u][:, c0 : c0 + nv, :], raw[i][:, :, 0:nv].rearrange("p e t -> p t e")
+            )
+            nc.scalar.activation(
+                pairs[u][:, c0 + nv : c0 + n, :], raw[i][:, :, nv:n].rearrange("p e t -> p t e"), COPY
+            )
+
+        cols = [keep.tile([P, EH, 4], BF16, name=f"cols{h}", align_bytes=64) for h in range(HALVES)]
+        cols_flat = [t[:].rearrange("p c j -> p (c j)") for t in cols]
+        cols_words = [t.bitcast(U32).rearrange("p (c u) -> p c u", u=2) for t in cols_flat]
+
+        def gather(u, h):
+            n = EH // 16
+            nc.vector.tensor_copy(cols_words[h][:, :, u], words[u].indirect(lists[:, h * n : (h + 1) * n]))
+
+        cast(0)
+        cast(1)
+        w_bf = keep.tile([P, M, 4], BF16, name="w_bf", align_bytes=64)
+        nc.scalar.activation(w_bf[:], w_raw[:].rearrange("p j m -> p m j"), COPY)
+        gather(0, 0)
+        gather(0, 1)
+        w_codes = keep.tile([P, M], U32, name="w_codes", align_bytes=64)
+        w_scales = keep.tile([P, M], U8, name="w_scales", align_bytes=64)
+        nc.vector.quantize_mx(
+            out=w_codes[:].bitcast(FP8X4), scales=w_scales[:], in_=w_bf[:].rearrange("p m j -> p (m j)")
+        )
+        cast(2)
+        cast(3)
+        cast(4)
+        gather(1, 0)
+        gather(1, 1)
+
+        codes = []
+        scales = []
+        for h in range(HALVES):
+            q = keep.tile([P, EH], U32, name=f"codes{h}", align_bytes=64)
+            s = keep.tile([P, EH], U8, name=f"scales{h}", align_bytes=64)
+            nc.vector.quantize_mx(out=q[:].bitcast(FP8X4), scales=s[:], in_=cols_flat[h])
+            codes.append(q)
+            scales.append(s)
+        for h in range(HALVES):
+            y = keep.tile([P, M // P, GH], F32, name=f"y{h}")
+            for a in range(M // P):
+                acc = psum.tile([P, EH], F32, name=f"acc{h}{a}")
+                nc.tensor.matmul_mx(
+                    out=acc[:],
+                    lhsT=w_codes[:, a * P : (a + 1) * P].bitcast(FP8X4),
+                    lhsT_scale=w_scales[:, a * P : (a + 1) * P],
+                    rhs=codes[h][:].bitcast(FP8X4),
+                    rhs_scale=scales[h][:],
+                    start=True,
+                    stop=True,
+                )
+                nc.vector.tensor_reduce(y[:, a, :], acc[:].rearrange("p (g j) -> p g j", j=NB), AXIS_X, MAX)
+            nc.sync.dma_start(out_rows[:, :, h * GH : (h + 1) * GH], y[:])

@@ -18,8 +18,10 @@ COPY = mybir.ActivationFunctionType.Copy
 MAX = mybir.AluOpType.max
 AXIS_X = mybir.AxisListType.X
 
+PIECES = 4
+EP = E // PIECES
+GP = G // PIECES
 HALVES = 2
-EH = E // HALVES
 GH = G // HALVES
 
 
@@ -32,7 +34,7 @@ def tile_attend_edge_kernel(tc, xT, w, offs, out):
     chunks = [
         (0, 0, 1024, 640),
         (0, 1024, 1024, 640),
-        (1, 0, 1024, 640),
+        (1, 0, 1024, 512),
         (1, 1024, 512, 320),
         (1, 1536, 512, 320),
     ]
@@ -58,58 +60,83 @@ def tile_attend_edge_kernel(tc, xT, w, offs, out):
 
         def cast(i):
             u, c0, n, nv = chunks[i]
-            nc.vector.tensor_copy(
-                pairs[u][:, c0 : c0 + nv, :], raw[i][:, :, 0:nv].rearrange("p e t -> p t e")
-            )
-            nc.scalar.activation(
-                pairs[u][:, c0 + nv : c0 + n, :], raw[i][:, :, nv:n].rearrange("p e t -> p t e"), COPY
-            )
+            if nv > 0:
+                nc.vector.tensor_copy(
+                    pairs[u][:, c0 : c0 + nv, :], raw[i][:, :, 0:nv].rearrange("p e t -> p t e")
+                )
+            if nv < n:
+                nc.scalar.activation(
+                    pairs[u][:, c0 + nv : c0 + n, :], raw[i][:, :, nv:n].rearrange("p e t -> p t e"), COPY
+                )
 
-        cols = [keep.tile([P, EH, 4], BF16, name=f"cols{h}", align_bytes=64) for h in range(HALVES)]
+        cols = [keep.tile([P, EP, 4], BF16, name=f"cols{q}", align_bytes=64) for q in range(PIECES)]
         cols_flat = [t[:].rearrange("p c j -> p (c j)") for t in cols]
         cols_words = [t.bitcast(U32).rearrange("p (c u) -> p c u", u=2) for t in cols_flat]
+        late = [keep.tile([P, EP, 2], BF16, name=f"late{q}") for q in range(PIECES)]
 
-        def gather(u, h):
-            n = EH // 16
-            nc.vector.tensor_copy(cols_words[h][:, :, u], words[u].indirect(lists[:, h * n : (h + 1) * n]))
+        def picked(u, q):
+            return words[u].indirect(lists[:, q * (EP // 16) : (q + 1) * (EP // 16)])
 
-        cast(0)
-        cast(1)
+        for i in range(len(chunks)):
+            if chunks[i][0] == 0:
+                cast(i)
         w_bf = keep.tile([P, M, 4], BF16, name="w_bf", align_bytes=64)
         nc.scalar.activation(w_bf[:], w_raw[:].rearrange("p j m -> p m j"), COPY)
-        gather(0, 0)
-        gather(0, 1)
+        for q in range(PIECES):
+            nc.vector.tensor_copy(cols_words[q][:, :, 0], picked(0, q))
         w_codes = keep.tile([P, M], U32, name="w_codes", align_bytes=64)
         w_scales = keep.tile([P, M], U8, name="w_scales", align_bytes=64)
         nc.vector.quantize_mx(
             out=w_codes[:].bitcast(FP8X4), scales=w_scales[:], in_=w_bf[:].rearrange("p m j -> p (m j)")
         )
-        cast(2)
-        cast(3)
-        cast(4)
-        gather(1, 0)
-        gather(1, 1)
+        for i in range(len(chunks)):
+            if chunks[i][0] == 1:
+                cast(i)
 
-        codes = []
-        scales = []
-        for h in range(HALVES):
-            q = keep.tile([P, EH], U32, name=f"codes{h}", align_bytes=64)
-            s = keep.tile([P, EH], U8, name=f"scales{h}", align_bytes=64)
-            nc.vector.quantize_mx(out=q[:].bitcast(FP8X4), scales=s[:], in_=cols_flat[h])
-            codes.append(q)
-            scales.append(s)
-        for h in range(HALVES):
-            y = keep.tile([P, M // P, GH], F32, name=f"y{h}")
+        for q in range(PIECES):
+            if q in []:
+                nc.vector.tensor_copy(cols_words[q][:, :, 1], picked(1, q))
+            else:
+                nc.vector.tensor_copy(late[q][:].rearrange("p c e -> p (c e)").bitcast(U32), picked(1, q))
+                nc.scalar.copy(cols[q][:, :, 2:4], late[q][:])
+
+        accs = []
+
+        def product(q):
+            codes = keep.tile([P, EP], U32, name=f"codes{q}", align_bytes=64)
+            scales = keep.tile([P, EP], U8, name=f"scales{q}", align_bytes=64)
+            nc.vector.quantize_mx(out=codes[:].bitcast(FP8X4), scales=scales[:], in_=cols_flat[q])
+            acc = psum.tile([P, M // P, EP], F32, name=f"acc{q}")
+            accs.append(acc)
             for a in range(M // P):
-                acc = psum.tile([P, EH], F32, name=f"acc{h}{a}")
                 nc.tensor.matmul_mx(
-                    out=acc[:],
+                    out=acc[:, a, :],
                     lhsT=w_codes[:, a * P : (a + 1) * P].bitcast(FP8X4),
                     lhsT_scale=w_scales[:, a * P : (a + 1) * P],
-                    rhs=codes[h][:].bitcast(FP8X4),
-                    rhs_scale=scales[h][:],
+                    rhs=codes[:].bitcast(FP8X4),
+                    rhs_scale=scales[:],
                     start=True,
                     stop=True,
                 )
-                nc.vector.tensor_reduce(y[:, a, :], acc[:].rearrange("p (g j) -> p g j", j=NB), AXIS_X, MAX)
-            nc.sync.dma_start(out_rows[:, :, h * GH : (h + 1) * GH], y[:])
+
+        ys = [keep.tile([P, M // P, GH], F32, name=f"y{h}") for h in range(HALVES)]
+
+        def largest(q):
+            h, r = divmod(q, PIECES // HALVES)
+            nc.vector.tensor_reduce(
+                ys[h][:, :, r * GP : (r + 1) * GP],
+                accs[q][:].rearrange("p a (g j) -> p a g j", j=NB),
+                AXIS_X,
+                MAX,
+            )
+            if r == PIECES // HALVES - 1:
+                nc.sync.dma_start(out_rows[:, :, h * GH : (h + 1) * GH], ys[h][:])
+
+        product(0)
+        product(1)
+        largest(0)
+        product(2)
+        largest(1)
+        product(3)
+        largest(2)
+        largest(3)

@@ -32,11 +32,11 @@ def tile_attend_edge_kernel(tc, xT, w, offs, out):
     out_rows = out.rearrange("(a p) g -> p a g", p=P)
 
     chunks = [
-        (0, 0, 1024, 640),
-        (0, 1024, 1024, 640),
-        (1, 0, 1024, 512),
-        (1, 1024, 512, 320),
-        (1, 1536, 512, 320),
+        (0, 0, 1536, 1088),
+        (0, 1536, 512, 320),
+        (1, 0, 1024, 256),
+        (1, 1024, 768, 448),
+        (1, 1792, 256, 160),
     ]
 
     with ExitStack() as ctx:
@@ -52,65 +52,55 @@ def tile_attend_edge_kernel(tc, xT, w, offs, out):
             nc.sync.dma_start(r[:], x_rows[:, 2 * u : 2 * u + 2, c0 : c0 + n])
             if i == 0:
                 nc.sync.dma_start(lists[:], offs)
-            if i == 1:
-                nc.sync.dma_start(w_raw[:], w_rows)
+        nc.sync.dma_start(w_raw[:], w_rows)
 
         pairs = [keep.tile([P, T, 2], BF16, name=f"pairs{u}") for u in range(2)]
         words = [t[:].rearrange("p t e -> p (t e)").bitcast(U32) for t in pairs]
 
         def cast(i):
             u, c0, n, nv = chunks[i]
-            if nv > 0:
-                nc.vector.tensor_copy(
-                    pairs[u][:, c0 : c0 + nv, :], raw[i][:, :, 0:nv].rearrange("p e t -> p t e")
-                )
-            if nv < n:
-                nc.scalar.activation(
-                    pairs[u][:, c0 + nv : c0 + n, :], raw[i][:, :, nv:n].rearrange("p e t -> p t e"), COPY
-                )
+            nc.vector.tensor_copy(
+                pairs[u][:, c0 : c0 + nv, :], raw[i][:, :, 0:nv].rearrange("p e t -> p t e")
+            )
+            nc.scalar.activation(
+                pairs[u][:, c0 + nv : c0 + n, :], raw[i][:, :, nv:n].rearrange("p e t -> p t e"), COPY
+            )
 
         cols = [keep.tile([P, EP, 4], BF16, name=f"cols{q}", align_bytes=64) for q in range(PIECES)]
         cols_flat = [t[:].rearrange("p c j -> p (c j)") for t in cols]
         cols_words = [t.bitcast(U32).rearrange("p (c u) -> p c u", u=2) for t in cols_flat]
-        late = [keep.tile([P, EP, 2], BF16, name=f"late{q}") for q in range(PIECES)]
 
-        def picked(u, q):
-            return words[u].indirect(lists[:, q * (EP // 16) : (q + 1) * (EP // 16)])
+        def gather(u, q, late):
+            picked = words[u].indirect(lists[:, q * (EP // 16) : (q + 1) * (EP // 16)])
+            if late:
+                dense = keep.tile([P, EP, 2], BF16, name=f"dense{u}{q}")
+                nc.vector.tensor_copy(dense[:].rearrange("p c e -> p (c e)").bitcast(U32), picked)
+                nc.scalar.copy(cols[q][:, :, 2 * u : 2 * u + 2], dense[:])
+            else:
+                nc.vector.tensor_copy(cols_words[q][:, :, u], picked)
 
-        for i in range(len(chunks)):
-            if chunks[i][0] == 0:
-                cast(i)
         w_bf = keep.tile([P, M, 4], BF16, name="w_bf", align_bytes=64)
-        nc.scalar.activation(w_bf[:], w_raw[:].rearrange("p j m -> p m j"), COPY)
-        for q in range(PIECES):
-            nc.vector.tensor_copy(cols_words[q][:, :, 0], picked(0, q))
         w_codes = keep.tile([P, M], U32, name="w_codes", align_bytes=64)
         w_scales = keep.tile([P, M], U8, name="w_scales", align_bytes=64)
-        nc.vector.quantize_mx(
-            out=w_codes[:].bitcast(FP8X4), scales=w_scales[:], in_=w_bf[:].rearrange("p m j -> p (m j)")
-        )
-        for i in range(len(chunks)):
-            if chunks[i][0] == 1:
-                cast(i)
 
-        for q in range(PIECES):
-            if q in []:
-                nc.vector.tensor_copy(cols_words[q][:, :, 1], picked(1, q))
-            else:
-                nc.vector.tensor_copy(late[q][:].rearrange("p c e -> p (c e)").bitcast(U32), picked(1, q))
-                nc.scalar.copy(cols[q][:, :, 2:4], late[q][:])
+        def cast_w():
+            nc.vector.tensor_copy(w_bf[:], w_raw[:].rearrange("p j m -> p m j"))
 
-        accs = []
+        def quantize_w():
+            nc.vector.quantize_mx(
+                out=w_codes[:].bitcast(FP8X4), scales=w_scales[:], in_=w_bf[:].rearrange("p m j -> p (m j)")
+            )
+
+        accs = [None] * PIECES
 
         def product(q):
             codes = keep.tile([P, EP], U32, name=f"codes{q}", align_bytes=64)
             scales = keep.tile([P, EP], U8, name=f"scales{q}", align_bytes=64)
             nc.vector.quantize_mx(out=codes[:].bitcast(FP8X4), scales=scales[:], in_=cols_flat[q])
-            acc = psum.tile([P, M // P, EP], F32, name=f"acc{q}")
-            accs.append(acc)
+            accs[q] = psum.tile([P, M // P, EP], F32, name=f"acc{q}")
             for a in range(M // P):
                 nc.tensor.matmul_mx(
-                    out=acc[:, a, :],
+                    out=accs[q][:, a, :],
                     lhsT=w_codes[:, a * P : (a + 1) * P].bitcast(FP8X4),
                     lhsT_scale=w_scales[:, a * P : (a + 1) * P],
                     rhs=codes[:].bitcast(FP8X4),
@@ -132,11 +122,26 @@ def tile_attend_edge_kernel(tc, xT, w, offs, out):
             if r == PIECES // HALVES - 1:
                 nc.sync.dma_start(out_rows[:, :, h * GH : (h + 1) * GH], ys[h][:])
 
+        cast(0)
+        cast(1)
+        gather(0, 0, True)
+        gather(0, 1, False)
+        gather(0, 2, False)
+        gather(0, 3, False)
+        cast(2)
+        cast(3)
+        cast(4)
+        gather(1, 0, True)
+        gather(1, 1, True)
+        gather(1, 2, True)
+        cast_w()
+        gather(1, 3, True)
+        quantize_w()
         product(0)
         product(1)
-        largest(0)
         product(2)
-        largest(1)
         product(3)
+        largest(0)
+        largest(1)
         largest(2)
         largest(3)

@@ -18,10 +18,11 @@ COPY = mybir.ActivationFunctionType.Copy
 MAX = mybir.AluOpType.max
 AXIS_X = mybir.AxisListType.X
 
+HALVES = 2
+EH = E // HALVES
 PIECES = 4
 EP = E // PIECES
 GP = G // PIECES
-HALVES = 2
 GH = G // HALVES
 
 
@@ -31,53 +32,33 @@ def tile_attend_edge_kernel(tc, xT, w, offs, out):
     w_rows = w.rearrange("(p j) m -> p j m", j=4)
     out_rows = out.rearrange("(a p) g -> p a g", p=P)
 
-    chunks = [
-        (0, 0, 1536, 1088),
-        (0, 1536, 512, 320),
-        (1, 0, 1024, 256),
-        (1, 1024, 768, 448),
-        (1, 1792, 256, 160),
-    ]
-
     with ExitStack() as ctx:
         keep = ctx.enter_context(tc.tile_pool(name="keep", bufs=1))
         psum = ctx.enter_context(tc.psum_pool(name="psum", bufs=1))
 
         lists = keep.tile([P, E // 16], U16, name="lists")
+        nc.sync.dma_start(lists[:], offs)
+        tables = [keep.tile([P, T], F32, name=f"table{t}") for t in range(4)]
+        for t in range(4):
+            nc.sync.dma_start(tables[t][:], x_rows[:, t, :])
         w_raw = keep.tile([P, 4, M], F32, name="w_raw")
-        raw = []
-        for i, (u, c0, n, nv) in enumerate(chunks):
-            r = keep.tile([P, 2, n], F32, name=f"raw{i}")
-            raw.append(r)
-            nc.sync.dma_start(r[:], x_rows[:, 2 * u : 2 * u + 2, c0 : c0 + n])
-            if i == 0:
-                nc.sync.dma_start(lists[:], offs)
         nc.sync.dma_start(w_raw[:], w_rows)
 
-        pairs = [keep.tile([P, T, 2], BF16, name=f"pairs{u}") for u in range(2)]
-        words = [t[:].rearrange("p t e -> p (t e)").bitcast(U32) for t in pairs]
+        dense = [[keep.tile([P, 2, EH], F32, name=f"dense{u}{h}") for h in range(HALVES)] for u in range(2)]
+        cols = [keep.tile([P, EH, 4], BF16, name=f"cols{h}", align_bytes=64) for h in range(HALVES)]
 
-        def cast(i):
-            u, c0, n, nv = chunks[i]
+        def gather(t, first, n):
+            u, e = divmod(t, 2)
+            h, c = divmod(first, EH)
             nc.vector.tensor_copy(
-                pairs[u][:, c0 : c0 + nv, :], raw[i][:, :, 0:nv].rearrange("p e t -> p t e")
-            )
-            nc.scalar.activation(
-                pairs[u][:, c0 + nv : c0 + n, :], raw[i][:, :, nv:n].rearrange("p e t -> p t e"), COPY
+                dense[u][h][:, e, c : c + n], tables[t][:].indirect(lists[:, first // 16 : (first + n) // 16])
             )
 
-        cols = [keep.tile([P, EP, 4], BF16, name=f"cols{q}", align_bytes=64) for q in range(PIECES)]
-        cols_flat = [t[:].rearrange("p c j -> p (c j)") for t in cols]
-        cols_words = [t.bitcast(U32).rearrange("p (c u) -> p c u", u=2) for t in cols_flat]
-
-        def gather(u, q, late):
-            picked = words[u].indirect(lists[:, q * (EP // 16) : (q + 1) * (EP // 16)])
-            if late:
-                dense = keep.tile([P, EP, 2], BF16, name=f"dense{u}{q}")
-                nc.vector.tensor_copy(dense[:].rearrange("p c e -> p (c e)").bitcast(U32), picked)
-                nc.scalar.copy(cols[q][:, :, 2 * u : 2 * u + 2], dense[:])
-            else:
-                nc.vector.tensor_copy(cols_words[q][:, :, u], picked)
+        def weave(u, first, n):
+            h, c = divmod(first, EH)
+            nc.scalar.copy(
+                cols[h][:, c : c + n, 2 * u : 2 * u + 2], dense[u][h][:, :, c : c + n].rearrange("p e c -> p c e")
+            )
 
         w_bf = keep.tile([P, M, 4], BF16, name="w_bf", align_bytes=64)
         w_codes = keep.tile([P, M], U32, name="w_codes", align_bytes=64)
@@ -94,9 +75,14 @@ def tile_attend_edge_kernel(tc, xT, w, offs, out):
         accs = [None] * PIECES
 
         def product(q):
+            h, r = divmod(q, PIECES // HALVES)
             codes = keep.tile([P, EP], U32, name=f"codes{q}", align_bytes=64)
             scales = keep.tile([P, EP], U8, name=f"scales{q}", align_bytes=64)
-            nc.vector.quantize_mx(out=codes[:].bitcast(FP8X4), scales=scales[:], in_=cols_flat[q])
+            nc.vector.quantize_mx(
+                out=codes[:].bitcast(FP8X4),
+                scales=scales[:],
+                in_=cols[h][:].rearrange("p c j -> p (c j)")[:, 4 * r * EP : 4 * (r + 1) * EP],
+            )
             accs[q] = psum.tile([P, M // P, EP], F32, name=f"acc{q}")
             for a in range(M // P):
                 nc.tensor.matmul_mx(
@@ -122,20 +108,17 @@ def tile_attend_edge_kernel(tc, xT, w, offs, out):
             if r == PIECES // HALVES - 1:
                 nc.sync.dma_start(out_rows[:, :, h * GH : (h + 1) * GH], ys[h][:])
 
-        cast(0)
-        cast(1)
-        gather(0, 0, True)
-        gather(0, 1, False)
-        gather(0, 2, False)
-        gather(0, 3, False)
-        cast(2)
-        cast(3)
-        cast(4)
-        gather(1, 0, True)
-        gather(1, 1, True)
-        gather(1, 2, True)
+        for h in range(HALVES):
+            gather(0, h * EH, EH)
+        for h in range(HALVES):
+            gather(1, h * EH, EH)
+            weave(0, h * EH, EH)
+        for h in range(HALVES):
+            gather(2, h * EH, EH)
+        for q in range(PIECES):
+            gather(3, q * EP, EP)
+            weave(1, q * EP, EP)
         cast_w()
-        gather(1, 3, True)
         quantize_w()
         product(0)
         product(1)

from contextlib import ExitStack

import concourse.mybir as mybir

D, T, M = 512, 2048, 256
G, NB = 64, 16
E = G * NB
P = 128
FLOPS = 2 * D * M * E

F32 = mybir.dt.float32
BF16 = mybir.dt.bfloat16
U32 = mybir.dt.uint32
U16 = mybir.dt.uint16
U8 = mybir.dt.uint8
FP8X4 = mybir.dt.float8_e4m3fn_x4
COPY = mybir.ActivationFunctionType.Copy
MAX = mybir.AluOpType.max
AXIS_X = mybir.AxisListType.X

HALVES = 2
EH = E // HALVES
PIECES = 4
EP = E // PIECES
GP = G // PIECES
GH = G // HALVES


def tile_attend_edge_kernel(tc, xT, w, offs, out):
    nc = tc.nc
    x_rows = xT.rearrange("(p j) t -> p j t", j=4)
    w_rows = w.rearrange("(p j) m -> p j m", j=4)
    out_rows = out.rearrange("(a p) g -> p a g", p=P)

    with ExitStack() as ctx:
        keep = ctx.enter_context(tc.tile_pool(name="keep", bufs=1))
        psum = ctx.enter_context(tc.psum_pool(name="psum", bufs=1))

        lists = keep.tile([P, E // 16], U16, name="lists")
        nc.sync.dma_start(lists[:], offs)
        tables = [keep.tile([P, T], F32, name=f"table{t}") for t in range(4)]
        for t in range(4):
            nc.sync.dma_start(tables[t][:], x_rows[:, t, :])
        w_raw = keep.tile([P, 4, M], F32, name="w_raw")
        nc.sync.dma_start(w_raw[:], w_rows)

        dense = [[keep.tile([P, 2, EH], F32, name=f"dense{u}{h}") for h in range(HALVES)] for u in range(2)]
        cols = [keep.tile([P, EH, 4], BF16, name=f"cols{h}", align_bytes=64) for h in range(HALVES)]

        def gather(t, first, n):
            u, e = divmod(t, 2)
            h, c = divmod(first, EH)
            nc.vector.tensor_copy(
                dense[u][h][:, e, c : c + n], tables[t][:].indirect(lists[:, first // 16 : (first + n) // 16])
            )

        def weave(u, first, n):
            h, c = divmod(first, EH)
            nc.scalar.copy(
                cols[h][:, c : c + n, 2 * u : 2 * u + 2], dense[u][h][:, :, c : c + n].rearrange("p e c -> p c e")
            )

        w_bf = keep.tile([P, M, 4], BF16, name="w_bf", align_bytes=64)
        w_codes = keep.tile([P, M], U32, name="w_codes", align_bytes=64)
        w_scales = keep.tile([P, M], U8, name="w_scales", align_bytes=64)

        def cast_w():
            nc.vector.tensor_copy(w_bf[:], w_raw[:].rearrange("p j m -> p m j"))

        def quantize_w():
            nc.vector.quantize_mx(
                out=w_codes[:].bitcast(FP8X4), scales=w_scales[:], in_=w_bf[:].rearrange("p m j -> p (m j)")
            )

        accs = [None] * PIECES

        def product(q):
            h, r = divmod(q, PIECES // HALVES)
            codes = keep.tile([P, EP], U32, name=f"codes{q}", align_bytes=64)
            scales = keep.tile([P, EP], U8, name=f"scales{q}", align_bytes=64)
            nc.vector.quantize_mx(
                out=codes[:].bitcast(FP8X4),
                scales=scales[:],
                in_=cols[h][:].rearrange("p c j -> p (c j)")[:, 4 * r * EP : 4 * (r + 1) * EP],
            )
            accs[q] = psum.tile([P, M // P, EP], F32, name=f"acc{q}")
            for a in range(M // P):
                nc.tensor.matmul_mx(
                    out=accs[q][:, a, :],
                    lhsT=w_codes[:, a * P : (a + 1) * P].bitcast(FP8X4),
                    lhsT_scale=w_scales[:, a * P : (a + 1) * P],
                    rhs=codes[:].bitcast(FP8X4),
                    rhs_scale=scales[:],
                    start=True,
                    stop=True,
                )

        ys = [keep.tile([P, M // P, GH], F32, name=f"y{h}") for h in range(HALVES)]

        def largest(q):
            h, r = divmod(q, PIECES // HALVES)
            nc.vector.tensor_reduce(
                ys[h][:, :, r * GP : (r + 1) * GP],
                accs[q][:].rearrange("p a (g j) -> p a g j", j=NB),
                AXIS_X,
                MAX,
            )
            if r == PIECES // HALVES - 1:
                nc.sync.dma_start(out_rows[:, :, h * GH : (h + 1) * GH], ys[h][:])

        for h in range(HALVES):
            gather(0, h * EH, EH)
        for h in range(HALVES):
            gather(1, h * EH, EH)
            weave(0, h * EH, EH)
        for h in range(HALVES):
            gather(2, h * EH, EH)
        for q in range(PIECES):
            gather(3, q * EP, EP)
            weave(1, q * EP, EP)
        cast_w()
        quantize_w()
        product(0)
        product(1)
        product(2)
        product(3)
        largest(0)
        largest(1)
        largest(2)
        largest(3)
